import numpy as np
import ml_dtypes


def mxq(x, axis, fmt="e4m3"):
    dtype, down = {"e4m3": (ml_dtypes.float8_e4m3fn, 7), "e5m2": (ml_dtypes.float8_e5m2, 14)}[fmt]
    v = np.moveaxis(np.asarray(x, np.float32).astype(ml_dtypes.bfloat16).astype(np.float64), axis, -1)
    blocks = v.reshape(v.shape[:-1] + (-1, 32))
    amax = np.abs(blocks).max(-1, keepdims=True)
    byte = np.maximum(np.where(amax > 0, np.frexp(amax)[1] - 1 + 127, 0) - down, 1)
    scale = np.exp2(byte - 127.0)
    codes = (blocks / scale).astype(np.float32).astype(dtype).astype(np.float64)
    return np.moveaxis((codes * scale).reshape(v.shape), -1, axis)


WIDE = False


def mx_kscale(k):
    if not WIDE:
        return np.ones(k)
    levels = np.array([10, -10, 5, -5, 0])
    if k % 512:
        return np.exp2(np.random.permutation(np.resize(levels, k // 32))).repeat(32)
    a = np.empty((k // 512, 16))
    for p in range(k // 512):
        a[p, :8] = np.random.permutation(np.resize(levels, 8))
        for g in range(8):
            far = levels[np.abs(levels - a[p, g]) >= 10]
            a[p, g + 8] = far[np.random.randint(len(far))]
    return np.exp2(a.ravel()).repeat(32)


BF16 = ml_dtypes.bfloat16


def bf(x):
    return np.asarray(x, np.float32).astype(BF16)


def f64(x):
    return np.asarray(x).astype(np.float64)


E2M1 = np.array([0.0, 0.5, 1.0, 1.5, 2.0, 3.0, 4.0, 6.0, -0.0, -0.5, -1.0, -1.5, -2.0, -3.0, -4.0, -6.0])


def pack_weight(w, fmt):
    k, n = w.shape
    w = f64(bf(w)).reshape(k // 32, 32, n)
    amax = np.abs(w).max(1)
    if fmt == "e4m3":
        byte = np.frexp(amax)[1] - 1 + 127 - 7
    else:
        mant, ex = np.frexp(amax / 6.0)
        byte = np.where(mant > 0.5, ex, ex - 1) + 127
    byte = np.clip(np.where(amax > 0, byte, 1), 1, 254)
    scaled = (w * np.exp2(127.0 - byte)[:, None, :]).reshape(k, n).astype(np.float32)
    by_word = np.ascontiguousarray(scaled.reshape(k // 512, 128, 4, n).transpose(0, 1, 3, 2))
    if fmt == "e4m3":
        words = by_word.astype(ml_dtypes.float8_e4m3fn).view(np.uint8)
    else:
        c = by_word.astype(ml_dtypes.float4_e2m1fn).view(np.uint8) & 0xF
        words = c[..., 0::2] | (c[..., 1::2] << 4)
    return np.ascontiguousarray(words), np.ascontiguousarray(byte.astype(np.uint8).reshape(k // 512, 16, n))


def unpack_weight(words, scales, fmt):
    g, p, n, _ = words.shape
    if fmt == "e4m3":
        vals = np.ascontiguousarray(words).view(ml_dtypes.float8_e4m3fn).astype(np.float64)
    else:
        nib = np.empty((g, p, n, 4), np.uint8)
        nib[..., 0::2] = words & 0xF
        nib[..., 1::2] = words >> 4
        vals = E2M1[nib]
    vals = vals * np.repeat(np.exp2(scales.astype(np.float64) - 127.0), 8, axis=1)[..., None]
    return vals.transpose(0, 1, 3, 2).reshape(g * 512, n)
def pack4(w):
    words, scales = pack_weight(w, "e2m1")
    return words.reshape(words.shape[0], 128, -1), scales


def unpack4(words, scales):
    return unpack_weight(words.reshape(words.shape[0], 128, -1, 2), scales, "e2m1")


def planes(Y):
    n, m = Y.shape
    b = f64(bf(Y)).reshape(n // 32, 32, m)
    amax = np.abs(b).max(1)
    byte = np.clip(np.where(amax > 0, np.frexp(amax)[1] - 1 + 127 - 7, 1), 1, 254)
    codes = (b * np.exp2(127.0 - byte)[:, None, :]).reshape(n, m).astype(np.float32).astype(ml_dtypes.float8_e4m3fn).view(np.uint8)
    words = codes.reshape(n // 512, 128, 4, m).transpose(0, 1, 3, 2)
    return np.ascontiguousarray(words), np.ascontiguousarray(byte.astype(np.uint8).reshape(n // 512, 16, m))


R, C, K, N = 12, 128, 1536, 1024

def hankel(h):
    return h[np.arange(K)[:, None] + np.arange(N)[None, :]]

def setup_inputs():
    s = mx_kscale(K)
    x = np.random.randn(R, C, K) * s
    i = np.arange(K + N - 1)
    h = 1.5 * np.random.randn(K + N - 1) * np.exp(-i / (K + N)) / np.sqrt(K)
    hankel_words, hankel_scales = pack4(hankel(h) / s[:, None])
    bias = 0.5 * np.random.randn(C, N)
    lo = -0.8 - 0.4 * np.random.rand(N)
    hi = 0.8 + 0.4 * np.random.rand(N)
    gain = np.exp(0.8 * np.random.randn(N))
    return {"x": bf(x), "hankel_words": hankel_words, "hankel_scales": hankel_scales,
            "bias": bf(bias), "lo": bf(lo), "hi": bf(hi), "gain": bf(gain)}

def reference(x, hankel_words, hankel_scales, bias, lo, hi, gain):
    a = mxq(f64(x).reshape(R * C, K), 1, "e4m3")
    W = unpack4(hankel_words, hankel_scales)
    z = (a @ W).reshape(R, C, N)
    y = np.minimum(np.maximum(z + f64(bias), f64(lo)), f64(hi)) * f64(gain)
    Y = y.reshape(R * C, N).T
    words, scales = planes(Y)
    return y, words, scales

@@ -1,0 +1,349 @@
+from contextlib import ExitStack
+
+import concourse.mybir as mybir
+from concourse.masks import make_identity
+
+R, C, K, N = 12, 128, 1536, 1024
+FLOPS = 2 * R * C * K * N
+
+F32 = mybir.dt.float32
+BF16 = mybir.dt.bfloat16
+I32 = mybir.dt.int32
+U32 = mybir.dt.uint32
+U8 = mybir.dt.uint8
+FP8X4 = mybir.dt.float8_e4m3fn_x4
+FP4X4 = mybir.dt.float4_e2m1fn_x4
+ALU = mybir.AluOpType
+ACT = mybir.ActivationFunctionType
+
+P = 128
+PACK = 4
+GROUP = P * PACK
+KG = K // GROUP
+NG = N // GROUP
+RECS = 4
+CHUNKS = R // RECS
+COLS = RECS * C
+BANKS = 8
+
+
+def tile_hankel_clipped_response_g4_kernel(
+    tc, x, hankel_words, hankel_scales, bias, lo, hi, gain, out_0, out_1, out_2
+):
+    nc = tc.nc
+    with ExitStack() as ctx:
+        keep = ctx.enter_context(tc.tile_pool(name="keep", bufs=1))
+        work = ctx.enter_context(tc.tile_pool(name="work", bufs=4))
+        psum = ctx.enter_context(tc.psum_pool(name="psum", bufs=1))
+        ctx.enter_context(tc.manual_schedule())
+
+        banks_taken = []
+
+        def next_bank():
+            name = "bank%d" % (len(banks_taken) % BANKS)
+            banks_taken.append(name)
+            bank = psum.tile([P, COLS], F32, name=name, tag=name)
+            return bank
+
+        def kept(name, shape, dtype):
+            t = keep.tile(shape, dtype, name=name, tag=name, align_bytes=64)
+            return t
+
+        ident = kept("ident", [P, P], F32)
+        ws_raw = kept("ws_raw", [P, KG, N], U8)
+        w_raw = [kept("w_raw%d" % n, [P, KG, 2 * GROUP], U8) for n in range(NG)]
+        w_codes = [kept("w_codes%d" % n, [P, KG, PACK, 2 * P], U8) for n in range(NG)]
+        w_scales = [kept("w_scales%d" % n, [P, KG, PACK, P], U8) for n in range(NG)]
+        x_first = [kept("x_first%d" % g, [P, RECS, GROUP], BF16) for g in range(KG)]
+        x_pair = {q: kept("x_pair%d" % q, [P, 2, K], BF16) for q in range(2, R // 2)}
+        x_codes = {(j, g): kept("x_codes%d_%d" % (j, g), [P, COLS], U32) for j in range(CHUNKS) for g in range(KG)}
+        x_scales = {(j, g): kept("x_scales%d_%d" % (j, g), [P, COLS], U8) for j in range(CHUNKS) for g in range(KG)}
+        x_turned = {(j, g): kept("x_turned%d_%d" % (j, g), [P, COLS, 2], F32) for j in range(CHUNKS) for g in range(KG)}
+        bias_sb = kept("bias_sb", [P, N], BF16)
+        lo_sb = kept("lo_sb", [P, NG * PACK], BF16)
+        hi_sb = kept("hi_sb", [P, NG * PACK], BF16)
+        gain_sb = kept("gain_sb", [P, NG * PACK], BF16)
+        gain32 = kept("gain32", [P, NG * PACK], F32)
+        lo_eff = kept("lo_eff", [P, NG * PACK], F32)
+        end_a = kept("end_a", [P, NG * PACK], F32)
+        end_b = kept("end_b", [P, NG * PACK], F32)
+        lower = kept("lower", [P, NG * PACK], F32)
+        upper = kept("upper", [P, NG * PACK], F32)
+        gain_bias = kept("gain_bias", [P, NG * PACK, C], F32)
+        y_scales = [kept("y_scales%d" % j, [P, NG, COLS], U8) for j in range(CHUNKS)]
+
+        def by_lag(vec):
+            return vec.rearrange("(n p t) -> p n t", n=NG, t=PACK)
+
+        def load_vec(engine, tile, vec):
+            engine.dma_start(out=tile[:].rearrange("p (n t) -> p n t", t=PACK), in_=by_lag(vec))
+
+        def load_w(n):
+            src = hankel_words[:, :, 2 * GROUP * n : 2 * GROUP * (n + 1)].rearrange("g p b -> p g b")
+            nc.sync.dma_start(out=w_raw[n][:].bitcast(I32), in_=src.bitcast(I32))
+
+        def load_x_first(g):
+            src = x[0:RECS, :, GROUP * g : GROUP * (g + 1)].rearrange("r c k -> c r k")
+            nc.sync.dma_start(out=x_first[g][:], in_=src)
+
+        nc.vector.memset(ws_raw[:].rearrange("p g n -> p (g n)").bitcast(I32), 0)
+        make_identity(nc, ident[:])
+        load_vec(nc.scalar, gain_sb, gain)
+        load_x_first(0)
+        load_w(0)
+        for q in range(4):
+            src = hankel_scales[:, 4 * q : 4 * q + 4, :].rearrange("g r n -> r g n")
+            nc.sync.dma_start(out=ws_raw[32 * q : 32 * q + 4, :, :].bitcast(I32), in_=src.bitcast(I32))
+        load_x_first(1)
+        load_x_first(2)
+        nc.sync.dma_start(out=bias_sb[:], in_=bias)
+        load_w(1)
+        load_vec(nc.sync, lo_sb, lo)
+        load_vec(nc.sync, hi_sb, hi)
+        for q in range(2, R // 2):
+            nc.sync.dma_start(out=x_pair[q][:], in_=x[2 * q : 2 * q + 2, :, :].rearrange("r c k -> c r k"))
+
+        nc.scalar.activation(out=gain32[:], in_=gain_sb[:], func=ACT.Copy)
+
+        def x_words(rec, g):
+            if rec < RECS:
+                return x_first[g][:, rec, :].bitcast(F32)
+            return x_pair[rec // 2][:, rec % 2, GROUP * g : GROUP * (g + 1)].bitcast(F32)
+
+        def turn_x(q, g):
+            bank = next_bank()
+            for r in range(2):
+                words = x_words(2 * q + r, g)
+                for u in range(2):
+                    slot = 2 * r + u
+                    nc.tensor.transpose(bank[:, P * slot : P * (slot + 1)], words[:, u : 2 * P : 2], ident[:])
+            return bank
+
+        def empty_x(bank, q, g):
+            half = q % 2
+            dst = x_turned[(q // 2, g)][:, 2 * C * half : 2 * C * (half + 1), :]
+            nc.scalar.copy(
+                out=dst.rearrange("p (r c) u -> p r c u", r=2),
+                in_=bank[:].rearrange("p (r u c) -> p r c u", r=2, u=2),
+            )
+
+        def quantize_x(j, g, first, last):
+            cols = slice(first, last)
+            nc.vector.quantize_mx(
+                out=x_codes[(j, g)][:, cols].bitcast(FP8X4),
+                scales=x_scales[(j, g)][:, cols],
+                in_=x_turned[(j, g)][:, cols, :].rearrange("p m u -> p (m u)").bitcast(BF16),
+            )
+
+        def sort_w(n, g):
+            nc.vector.tensor_copy(
+                out=w_codes[n][:, g, :, :].rearrange("p t (m b) -> p t m b", b=2),
+                in_=w_raw[n][:, g, :].rearrange("p (m t b) -> p t m b", t=PACK, b=2),
+            )
+
+        def sort_ws(n):
+            nc.vector.tensor_copy(
+                out=w_scales[n][:],
+                in_=ws_raw[:, :, GROUP * n : GROUP * (n + 1)].rearrange("p g (m t) -> p g t m", t=PACK),
+            )
+
+        acc = {}
+        pre = {}
+        y_lag = {}
+        y_bf = {}
+        y_codes = {}
+
+        def mx_pass(h, t, g):
+            j, n = divmod(h, NG)
+            if g == 0:
+                acc[(h, t)] = next_bank()
+            nc.tensor.matmul_mx(
+                out=acc[(h, t)][:],
+                lhsT=w_codes[n][:, g, t, :].bitcast(FP4X4),
+                lhsT_scale=w_scales[n][:, g, t, :],
+                rhs=x_codes[(j, g)][:].bitcast(FP8X4),
+                rhs_scale=x_scales[(j, g)][:],
+                start=(g == 0),
+                stop=(g == KG - 1),
+            )
+
+        def mx_group(h, t):
+            for g in range(KG):
+                mx_pass(h, t, g)
+
+        def scale_add(h, t, first=0, last=RECS):
+            lag = PACK * (h % NG) + t
+            if (h, t) not in pre:
+                tile = work.tile([P, RECS, C], F32, name="pre", tag="pre")
+                pre[(h, t)] = tile
+            nc.vector.scalar_tensor_tensor(
+                out=pre[(h, t)][:, first:last, :],
+                in0=acc[(h, t)][:].rearrange("p (r c) -> p r c", r=RECS)[:, first:last, :],
+                scalar=gain32[:, lag : lag + 1],
+                in1=gain_bias[:, lag, :].unsqueeze(1).to_broadcast([P, last - first, C]),
+                op0=ALU.mult,
+                op1=ALU.add,
+            )
+
+        def clip(h, t, first=0, last=RECS):
+            lag = PACK * (h % NG) + t
+            if h not in y_lag:
+                tile = work.tile([P, PACK, COLS], F32, name="y_lag", tag="y_lag", bufs=3)
+                y_lag[h] = tile
+            nc.vector.tensor_scalar(
+                out=y_lag[h][:, t, C * first : C * last],
+                in0=pre[(h, t)][:, first:last, :].rearrange("p r c -> p (r c)"),
+                scalar1=upper[:, lag : lag + 1],
+                scalar2=lower[:, lag : lag + 1],
+                op0=ALU.min,
+                op1=ALU.max,
+            )
+
+        def turn_y(h, bank, r, t):
+            nc.tensor.transpose(bank[:, P * t : P * (t + 1)], y_lag[h][:, t, C * r : C * (r + 1)], ident[:])
+
+        def empty_y(copy, h, bank, r):
+            j, n = divmod(h, NG)
+            y_row = work.tile([P, GROUP], F32, name="y_row", tag="y_row", bufs=6)
+            copy(
+                out=y_row[:].rearrange("c (p t) -> c p t", t=PACK),
+                in_=bank[:].rearrange("c (t p) -> c p t", t=PACK),
+            )
+            nc.sync.dma_start(out=out_0[RECS * j + r, :, GROUP * n : GROUP * (n + 1)], in_=y_row[:])
+
+        def weave_y(copy, h, first, last):
+            if h not in y_bf:
+                tile = work.tile([P, COLS, PACK], BF16, name="y_bf", tag="y_bf", bufs=2, align_bytes=64)
+                y_bf[h] = tile
+            copy(
+                out=y_bf[h][:, first:last, :].rearrange("p (c i) t -> p c t i", i=4),
+                in_=y_lag[h][:, :, first:last].rearrange("p t (c i) -> p c t i", i=4),
+            )
+
+        def quantize_y(h):
+            j, n = divmod(h, NG)
+            codes = kept("y_codes%d" % h, [P, COLS], U32)
+            y_codes[h] = codes
+            nc.vector.quantize_mx(
+                out=codes[:].bitcast(FP8X4),
+                scales=y_scales[j][:, n, :],
+                in_=y_bf[h][:].rearrange("p m t -> p (m t)"),
+            )
+            dst = out_1[n, :, COLS * j : COLS * (j + 1), :].rearrange("p m t -> p (m t)")
+            nc.sync.dma_start(out=dst.bitcast(I32), in_=codes[:].bitcast(I32))
+            if n == NG - 1:
+                for q in range(4):
+                    dst = out_2[:, 4 * q : 4 * q + 4, COLS * j : COLS * (j + 1)].rearrange("n r m -> r n m")
+                    nc.sync.dma_start(out=dst.bitcast(I32), in_=y_scales[j][32 * q : 32 * q + 4, :, :].bitcast(I32))
+
+        for q in range(2):
+            empty_x(turn_x(q, 0), q, 0)
+        for g in range(KG):
+            sort_w(0, g)
+        sort_ws(0)
+        quantize_x(0, 0, 0, COLS)
+        sort_ws(1)
+        for q in range(2):
+            empty_x(turn_x(q, 1), q, 1)
+        quantize_x(0, 1, 0, COLS)
+        for q in range(2):
+            empty_x(turn_x(q, 2), q, 2)
+        bias_bank = next_bank()
+        bias_words = bias_sb[:].bitcast(F32)
+        for n in range(NG):
+            for u in range(2):
+                slot = 2 * n + u
+                nc.tensor.transpose(
+                    bias_bank[:, P * slot : P * (slot + 1)], bias_words[:, 2 * P * n + u : 2 * P * (n + 1) : 2], ident[:]
+                )
+        bias_by_lag = bias_bank[:].bitcast(BF16).rearrange("p (s c e) -> p s e c", c=C, e=2)
+        for lag in range(NG * PACK):
+            nc.scalar.activation(
+                out=gain_bias[:, lag, :],
+                in_=bias_by_lag[:, lag // 2, lag % 2, :],
+                func=ACT.Copy,
+                scale=gain32[:, lag : lag + 1],
+            )
+        sort_w(1, 0)
+        quantize_x(0, 2, 0, COLS)
+        nc.vector.tensor_tensor(out=lo_eff[:], in0=lo_sb[:], in1=hi_sb[:], op=ALU.min)
+        nc.vector.tensor_tensor(out=end_b[:], in0=hi_sb[:], in1=gain32[:], op=ALU.mult)
+        sort_w(1, 1)
+        nc.vector.tensor_tensor(out=end_a[:], in0=lo_eff[:], in1=gain32[:], op=ALU.mult)
+
+        halves = CHUNKS * NG
+        WEAVE_V = [128, 256, 256, 256, 256]
+        for h in range(halves - 1):
+            j = h // NG
+            if h == 0:
+                for t, g in [(0, 0), (0, 1), (1, 0), (1, 1), (0, 2), (2, 0), (1, 2), (2, 1), (2, 2), (3, 0), (3, 1), (3, 2)]:
+                    mx_pass(0, t, g)
+                scale_add(0, 0)
+                nc.vector.tensor_tensor(out=lower[:], in0=end_a[:], in1=end_b[:], op=ALU.min)
+                nc.vector.tensor_tensor(out=upper[:], in0=end_a[:], in1=end_b[:], op=ALU.max)
+                scale_add(0, 1)
+                clip(0, 0)
+                scale_add(0, 2)
+                clip(0, 1)
+                clip(0, 2)
+                scale_add(0, 3)
+                sort_w(1, 2)
+                clip(0, 3)
+            else:
+                for t in range(PACK):
+                    mx_group(h, t)
+                scale_add(h, 0)
+                scale_add(h, 1)
+                clip(h, 0)
+                scale_add(h, 2)
+                clip(h, 1)
+                quantize_y(h - 1)
+                scale_add(h, 3)
+                clip(h, 2)
+                clip(h, 3)
+            split = WEAVE_V[h]
+            if h < halves - 2:
+                q = h + 2
+                cols = (2 * C * (q % 2), 2 * C * (q % 2 + 1))
+                for g in range(KG):
+                    empty_x(turn_x(q, g), q, g)
+                quantize_x(q // 2, 0, *cols)
+                weave_y(nc.vector.tensor_copy, h, 0, split)
+                quantize_x(q // 2, 1, *cols)
+                quantize_x(q // 2, 2, *cols)
+            else:
+                mx_group(h + 1, 0)
+                mx_group(h + 1, 1)
+                weave_y(nc.scalar.copy, h, split, COLS)
+                scale_add(h + 1, 0)
+                weave_y(nc.vector.tensor_copy, h, 0, split)
+                scale_add(h + 1, 1)
+                clip(h + 1, 0)
+                quantize_y(h)
+                clip(h + 1, 1)
+            for r in range(RECS):
+                bank = next_bank()
+                for t in range(PACK):
+                    turn_y(h, bank, r, t)
+                empty_y(nc.scalar.copy, h, bank, r)
+            if h < halves - 2:
+                weave_y(nc.scalar.copy, h, split, COLS)
+
+        h = halves - 1
+        mx_group(h, 2)
+        mx_group(h, 3)
+        scale_add(h, 2)
+        scale_add(h, 3, 0, 2)
+        clip(h, 2)
+        scale_add(h, 3, 2, 4)
+        clip(h, 3, 0, 2)
+        clip(h, 3, 2, 4)
+        last_banks = [next_bank() for r in range(RECS)]
+        for t in range(PACK):
+            for r in range(RECS):
+                turn_y(h, last_banks[r], r, t)
+        weave_y(nc.vector.tensor_copy, h, 0, COLS)
+        for r in range(RECS - 1):
+            empty_y(nc.scalar.copy, h, last_banks[r], r)
+        quantize_y(h)
+        empty_y(nc.scalar.copy, h, last_banks[RECS - 1], RECS - 1)

@@ -37,13 +37,17 @@ def tile_hankel_clipped_response_g4_kernel(
         psum = ctx.enter_context(tc.psum_pool(name="psum", bufs=1))
         ctx.enter_context(tc.manual_schedule())
 
-        banks_taken = []
+        free_banks = ["bank%d" % b for b in range(BANKS)]
+        bank_names = {}
 
-        def next_bank():
-            name = "bank%d" % (len(banks_taken) % BANKS)
-            banks_taken.append(name)
+        def next_bank(key):
+            name = free_banks.pop(0)
+            bank_names[key] = name
             bank = psum.tile([P, COLS], F32, name=name, tag=name)
             return bank
+
+        def release(key):
+            free_banks.append(bank_names.pop(key))
 
         def kept(name, shape, dtype):
             t = keep.tile(shape, dtype, name=name, tag=name, align_bytes=64)
@@ -78,28 +82,35 @@ def tile_hankel_clipped_response_g4_kernel(
         def load_vec(engine, tile, vec):
             engine.dma_start(out=tile[:].rearrange("p (n t) -> p n t", t=PACK), in_=by_lag(vec))
 
-        def load_w(n):
-            src = hankel_words[:, :, 2 * GROUP * n : 2 * GROUP * (n + 1)].rearrange("g p b -> p g b")
-            nc.sync.dma_start(out=w_raw[n][:].bitcast(I32), in_=src.bitcast(I32))
+        def load_w(n, first, last):
+            src = hankel_words[first:last, :, 2 * GROUP * n : 2 * GROUP * (n + 1)].rearrange("g p b -> p g b")
+            nc.sync.dma_start(out=w_raw[n][:, first:last, :].bitcast(I32), in_=src.bitcast(I32))
 
-        def load_x_first(g):
-            src = x[0:RECS, :, GROUP * g : GROUP * (g + 1)].rearrange("r c k -> c r k")
-            nc.sync.dma_start(out=x_first[g][:], in_=src)
+        def load_x_first(g, first, last):
+            src = x[first:last, :, GROUP * g : GROUP * (g + 1)].rearrange("r c k -> c r k")
+            nc.sync.dma_start(out=x_first[g][:, first:last, :], in_=src)
+
+        def load_ws(n):
+            lags = slice(GROUP * n, GROUP * (n + 1))
+            for q in range(4):
+                src = hankel_scales[:, 4 * q : 4 * q + 4, lags].rearrange("g r n -> r g n")
+                nc.sync.dma_start(out=ws_raw[32 * q : 32 * q + 4, :, lags].bitcast(I32), in_=src.bitcast(I32))
 
         nc.vector.memset(ws_raw[:].rearrange("p g n -> p (g n)").bitcast(I32), 0)
         make_identity(nc, ident[:])
         load_vec(nc.scalar, gain_sb, gain)
-        load_x_first(0)
-        load_w(0)
-        for q in range(4):
-            src = hankel_scales[:, 4 * q : 4 * q + 4, :].rearrange("g r n -> r g n")
-            nc.sync.dma_start(out=ws_raw[32 * q : 32 * q + 4, :, :].bitcast(I32), in_=src.bitcast(I32))
-        load_x_first(1)
-        load_x_first(2)
+        load_x_first(0, 0, 2)
+        load_x_first(0, 2, RECS)
+        load_w(0, 0, 1)
+        load_x_first(1, 0, RECS)
+        load_ws(0)
+        load_w(0, 1, KG)
+        load_x_first(2, 0, RECS)
         nc.sync.dma_start(out=bias_sb[:], in_=bias)
-        load_w(1)
         load_vec(nc.sync, lo_sb, lo)
         load_vec(nc.sync, hi_sb, hi)
+        load_w(1, 0, KG)
+        load_ws(1)
         for q in range(2, R // 2):
             nc.sync.dma_start(out=x_pair[q][:], in_=x[2 * q : 2 * q + 2, :, :].rearrange("r c k -> c r k"))
 
@@ -111,7 +122,7 @@ def tile_hankel_clipped_response_g4_kernel(
             return x_pair[rec // 2][:, rec % 2, GROUP * g : GROUP * (g + 1)].bitcast(F32)
 
         def turn_x(q, g):
-            bank = next_bank()
+            bank = next_bank(("x", q, g))
             for r in range(2):
                 words = x_words(2 * q + r, g)
                 for u in range(2):
@@ -126,6 +137,7 @@ def tile_hankel_clipped_response_g4_kernel(
                 out=dst.rearrange("p (r c) u -> p r c u", r=2),
                 in_=bank[:].rearrange("p (r u c) -> p r c u", r=2, u=2),
             )
+            release(("x", q, g))
 
         def quantize_x(j, g, first, last):
             cols = slice(first, last)
@@ -141,10 +153,10 @@ def tile_hankel_clipped_response_g4_kernel(
                 in_=w_raw[n][:, g, :].rearrange("p (m t b) -> p t m b", t=PACK, b=2),
             )
 
-        def sort_ws(n):
+        def sort_ws(n, first, last):
             nc.vector.tensor_copy(
-                out=w_scales[n][:],
-                in_=ws_raw[:, :, GROUP * n : GROUP * (n + 1)].rearrange("p g (m t) -> p g t m", t=PACK),
+                out=w_scales[n][:, first:last, :, :],
+                in_=ws_raw[:, first:last, GROUP * n : GROUP * (n + 1)].rearrange("p g (m t) -> p g t m", t=PACK),
             )
 
         acc = {}
@@ -156,7 +168,7 @@ def tile_hankel_clipped_response_g4_kernel(
         def mx_pass(h, t, g):
             j, n = divmod(h, NG)
             if g == 0:
-                acc[(h, t)] = next_bank()
+                acc[(h, t)] = next_bank(("z", h, t))
             nc.tensor.matmul_mx(
                 out=acc[(h, t)][:],
                 lhsT=w_codes[n][:, g, t, :].bitcast(FP4X4),
@@ -184,6 +196,8 @@ def tile_hankel_clipped_response_g4_kernel(
                 op0=ALU.mult,
                 op1=ALU.add,
             )
+            if last == RECS:
+                release(("z", h, t))
 
         def clip(h, t, first=0, last=RECS):
             lag = PACK * (h % NG) + t
@@ -209,6 +223,7 @@ def tile_hankel_clipped_response_g4_kernel(
                 out=y_row[:].rearrange("c (p t) -> c p t", t=PACK),
                 in_=bank[:].rearrange("c (t p) -> c p t", t=PACK),
             )
+            release(("y", h, r))
             nc.sync.dma_start(out=out_0[RECS * j + r, :, GROUP * n : GROUP * (n + 1)], in_=y_row[:])
 
         def weave_y(copy, h, first, last):
@@ -220,35 +235,53 @@ def tile_hankel_clipped_response_g4_kernel(
                 in_=y_lag[h][:, :, first:last].rearrange("p t (c i) -> p c t i", i=4),
             )
 
-        def quantize_y(h):
+        def quantize_y(h, first=0, last=COLS):
             j, n = divmod(h, NG)
-            codes = kept("y_codes%d" % h, [P, COLS], U32)
-            y_codes[h] = codes
+            if h not in y_codes:
+                y_codes[h] = kept("y_codes%d" % h, [P, COLS], U32)
+            codes = y_codes[h][:, first:last]
             nc.vector.quantize_mx(
-                out=codes[:].bitcast(FP8X4),
-                scales=y_scales[j][:, n, :],
-                in_=y_bf[h][:].rearrange("p m t -> p (m t)"),
+                out=codes.bitcast(FP8X4),
+                scales=y_scales[j][:, n, first:last],
+                in_=y_bf[h][:, first:last, :].rearrange("p m t -> p (m t)"),
             )
-            dst = out_1[n, :, COLS * j : COLS * (j + 1), :].rearrange("p m t -> p (m t)")
-            nc.sync.dma_start(out=dst.bitcast(I32), in_=codes[:].bitcast(I32))
-            if n == NG - 1:
-                for q in range(4):
-                    dst = out_2[:, 4 * q : 4 * q + 4, COLS * j : COLS * (j + 1)].rearrange("n r m -> r n m")
-                    nc.sync.dma_start(out=dst.bitcast(I32), in_=y_scales[j][32 * q : 32 * q + 4, :, :].bitcast(I32))
+
+        def store_codes(h, first=0, last=COLS):
+            j, n = divmod(h, NG)
+            dst = out_1[n, :, COLS * j + first : COLS * j + last, :].rearrange("p m t -> p (m t)")
+            nc.sync.dma_start(out=dst.bitcast(I32), in_=y_codes[h][:, first:last].bitcast(I32))
+
+        def store_scales(j):
+            for q in range(4):
+                dst = out_2[:, 4 * q : 4 * q + 4, COLS * j : COLS * (j + 1)].rearrange("n r m -> r n m")
+                nc.sync.dma_start(out=dst.bitcast(I32), in_=y_scales[j][32 * q : 32 * q + 4, :, :].bitcast(I32))
+
+        def out_rows(h, records):
+            for r in records:
+                bank = next_bank(("y", h, r))
+                for t in range(PACK):
+                    turn_y(h, bank, r, t)
+                empty_y(nc.scalar.copy, h, bank, r)
+
+        def quantize_pair(q, g):
+            quantize_x(q // 2, g, 2 * C * (q % 2), 2 * C * (q % 2 + 1))
 
         for q in range(2):
             empty_x(turn_x(q, 0), q, 0)
-        for g in range(KG):
-            sort_w(0, g)
-        sort_ws(0)
+        sort_w(0, 0)
         quantize_x(0, 0, 0, COLS)
-        sort_ws(1)
+        sort_ws(0, 0, 1)
         for q in range(2):
             empty_x(turn_x(q, 1), q, 1)
+        sort_ws(0, 1, KG)
+        sort_w(0, 1)
         quantize_x(0, 1, 0, COLS)
+        sort_w(0, 2)
+        for t in range(PACK):
+            mx_pass(0, t, 0)
         for q in range(2):
             empty_x(turn_x(q, 2), q, 2)
-        bias_bank = next_bank()
+        bias_bank = next_bank("bias")
         bias_words = bias_sb[:].bitcast(F32)
         for n in range(NG):
             for u in range(2):
@@ -264,86 +297,111 @@ def tile_hankel_clipped_response_g4_kernel(
                 func=ACT.Copy,
                 scale=gain32[:, lag : lag + 1],
             )
-        sort_w(1, 0)
-        quantize_x(0, 2, 0, COLS)
+        release("bias")
         nc.vector.tensor_tensor(out=lo_eff[:], in0=lo_sb[:], in1=hi_sb[:], op=ALU.min)
         nc.vector.tensor_tensor(out=end_b[:], in0=hi_sb[:], in1=gain32[:], op=ALU.mult)
-        sort_w(1, 1)
+        sort_w(1, 0)
         nc.vector.tensor_tensor(out=end_a[:], in0=lo_eff[:], in1=gain32[:], op=ALU.mult)
+        sort_w(1, 1)
+        nc.vector.tensor_tensor(out=lower[:], in0=end_a[:], in1=end_b[:], op=ALU.min)
+        nc.vector.tensor_tensor(out=upper[:], in0=end_a[:], in1=end_b[:], op=ALU.max)
+        sort_w(1, 2)
+        quantize_x(0, 2, 0, COLS)
+        sort_ws(1, 0, KG)
+        turned = [(2, 0), (2, 1), (2, 2), (3, 0)]
+        for g in range(1, KG):
+            for t in range(PACK):
+                mx_pass(0, t, g)
+            for q, gx in turned[2 * g - 2 : 2 * g]:
+                empty_x(turn_x(q, gx), q, gx)
+        for t in range(PACK):
+            scale_add(0, t)
+        for t in range(PACK):
+            clip(0, t)
 
         halves = CHUNKS * NG
-        WEAVE_V = [128, 256, 256, 256, 256]
-        for h in range(halves - 1):
-            j = h // NG
-            if h == 0:
-                for t, g in [(0, 0), (0, 1), (1, 0), (1, 1), (0, 2), (2, 0), (1, 2), (2, 1), (2, 2), (3, 0), (3, 1), (3, 2)]:
-                    mx_pass(0, t, g)
-                scale_add(0, 0)
-                nc.vector.tensor_tensor(out=lower[:], in0=end_a[:], in1=end_b[:], op=ALU.min)
-                nc.vector.tensor_tensor(out=upper[:], in0=end_a[:], in1=end_b[:], op=ALU.max)
-                scale_add(0, 1)
-                clip(0, 0)
-                scale_add(0, 2)
-                clip(0, 1)
-                clip(0, 2)
-                scale_add(0, 3)
-                sort_w(1, 2)
-                clip(0, 3)
+        WV = 128
+        WM = (WV + COLS) // 2
+        for s in range(2, 2 * halves - 4):
+            h, odd = divmod(s, 2)
+            ta, tb = 2 * odd, 2 * odd + 1
+            mx_group(h, ta)
+            mx_group(h, tb)
+            if not odd:
+                weave_y(nc.scalar.copy, h - 1, WV, WM)
             else:
-                for t in range(PACK):
-                    mx_group(h, t)
-                scale_add(h, 0)
-                scale_add(h, 1)
-                clip(h, 0)
-                scale_add(h, 2)
-                clip(h, 1)
+                weave_y(nc.scalar.copy, h - 1, WM, COLS)
+            for q, g in turned:
+                quantize_pair(q, g)
+            scale_add(h, ta)
+            if not odd:
+                weave_y(nc.vector.tensor_copy, h - 1, 0, WV)
+            scale_add(h, tb)
+            clip(h, ta)
+            if odd:
                 quantize_y(h - 1)
-                scale_add(h, 3)
-                clip(h, 2)
-                clip(h, 3)
-            split = WEAVE_V[h]
-            if h < halves - 2:
-                q = h + 2
-                cols = (2 * C * (q % 2), 2 * C * (q % 2 + 1))
-                for g in range(KG):
-                    empty_x(turn_x(q, g), q, g)
-                quantize_x(q // 2, 0, *cols)
-                weave_y(nc.vector.tensor_copy, h, 0, split)
-                quantize_x(q // 2, 1, *cols)
-                quantize_x(q // 2, 2, *cols)
-            else:
-                mx_group(h + 1, 0)
-                mx_group(h + 1, 1)
-                weave_y(nc.scalar.copy, h, split, COLS)
-                scale_add(h + 1, 0)
-                weave_y(nc.vector.tensor_copy, h, 0, split)
-                scale_add(h + 1, 1)
-                clip(h + 1, 0)
-                quantize_y(h)
-                clip(h + 1, 1)
-            for r in range(RECS):
-                bank = next_bank()
-                for t in range(PACK):
-                    turn_y(h, bank, r, t)
-                empty_y(nc.scalar.copy, h, bank, r)
-            if h < halves - 2:
-                weave_y(nc.scalar.copy, h, split, COLS)
+                store_codes(h - 1)
+                if h % NG == 0:
+                    store_scales(h // NG - 1)
+            clip(h, tb)
+            j = h // NG + 1
+            todo = [(2 * j + i // KG, i % KG) for i in range(2 * KG)]
+            turned = todo[2 * (s % 4) : 2 * (s % 4) + 2]
+            for q, g in turned:
+                empty_x(turn_x(q, g), q, g)
+            out_rows(h - 1, [ta, tb])
 
+        h = halves - 2
+        mx_group(h, 0)
+        mx_group(h, 1)
+        weave_y(nc.scalar.copy, h - 1, WV, COLS)
+        weave_y(nc.vector.tensor_copy, h - 1, 0, WV)
+        scale_add(h, 0)
+        scale_add(h, 1)
+        clip(h, 0)
+        quantize_y(h - 1)
+        clip(h, 1)
+        out_rows(h - 1, range(2))
+        store_codes(h - 1)
+        store_scales(CHUNKS - 2)
+        out_rows(h - 1, range(2, RECS))
+        mx_group(h, 2)
+        mx_group(h, 3)
+        scale_add(h, 2)
+        clip(h, 2)
+        scale_add(h, 3)
+        clip(h, 3)
         h = halves - 1
+        mx_group(h, 0)
+        mx_group(h, 1)
+        weave_y(nc.scalar.copy, h - 1, 192, COLS)
+        scale_add(h, 0)
+        weave_y(nc.vector.tensor_copy, h - 1, 0, 192)
+        scale_add(h, 1)
+        clip(h, 0)
+        quantize_y(h - 1)
+        clip(h, 1)
+        out_rows(h - 1, range(1))
+        store_codes(h - 1)
+        out_rows(h - 1, range(1, RECS))
         mx_group(h, 2)
         mx_group(h, 3)
         scale_add(h, 2)
         scale_add(h, 3, 0, 2)
         clip(h, 2)
-        scale_add(h, 3, 2, 4)
         clip(h, 3, 0, 2)
+        scale_add(h, 3, 2, 4)
         clip(h, 3, 2, 4)
-        last_banks = [next_bank() for r in range(RECS)]
+        last_banks = [next_bank(("y", h, r)) for r in range(RECS)]
         for t in range(PACK):
             for r in range(RECS):
                 turn_y(h, last_banks[r], r, t)
-        weave_y(nc.vector.tensor_copy, h, 0, COLS)
-        for r in range(RECS - 1):
-            empty_y(nc.scalar.copy, h, last_banks[r], r)
+        empty_y(nc.scalar.copy, h, last_banks[0], 0)
+        empty_y(nc.scalar.copy, h, last_banks[1], 1)
+        weave_y(nc.vector.tensor_copy, h, 0, COLS // 2)
+        weave_y(nc.vector.tensor_copy, h, COLS // 2, COLS)
         quantize_y(h)
-        empty_y(nc.scalar.copy, h, last_banks[RECS - 1], RECS - 1)
+        empty_y(nc.scalar.copy, h, last_banks[2], 2)
+        store_codes(h)
+        empty_y(nc.scalar.copy, h, last_banks[3], 3)
+        store_scales(CHUNKS - 1)

@@ -101,8 +101,9 @@ def tile_hankel_clipped_response_g4_kernel(
         load_vec(nc.scalar, gain_sb, gain)
         load_x_first(0, 0, 2)
         load_x_first(0, 2, RECS)
+        load_x_first(1, 0, 2)
         load_w(0, 0, 1)
-        load_x_first(1, 0, RECS)
+        load_x_first(1, 2, RECS)
         load_ws(0)
         load_w(0, 1, KG)
         load_x_first(2, 0, RECS)
@@ -121,13 +122,24 @@ def tile_hankel_clipped_response_g4_kernel(
                 return x_first[g][:, rec, :].bitcast(F32)
             return x_pair[rec // 2][:, rec % 2, GROUP * g : GROUP * (g + 1)].bitcast(F32)
 
+        x_parted = {}
+
+        def part_x(copy, q, g):
+            tile = work.tile([P, 2, 2, P], F32, name="x_parted", tag="x_parted", bufs=4)
+            x_parted[(q, g)] = tile
+            words = x_pair[q][:, :, GROUP * g : GROUP * (g + 1)].bitcast(F32)
+            copy(out=tile[:], in_=words.rearrange("c r (p u) -> c r u p", u=2))
+
         def turn_x(q, g):
             bank = next_bank(("x", q, g))
             for r in range(2):
-                words = x_words(2 * q + r, g)
                 for u in range(2):
                     slot = 2 * r + u
-                    nc.tensor.transpose(bank[:, P * slot : P * (slot + 1)], words[:, u : 2 * P : 2], ident[:])
+                    if (q, g) in x_parted:
+                        words = x_parted[(q, g)][:, r, u, :]
+                    else:
+                        words = x_words(2 * q + r, g)[:, u : 2 * P : 2]
+                    nc.tensor.transpose(bank[:, P * slot : P * (slot + 1)], words, ident[:])
             return bank
 
         def empty_x(bank, q, g):
@@ -269,7 +281,8 @@ def tile_hankel_clipped_response_g4_kernel(
         for q in range(2):
             empty_x(turn_x(q, 0), q, 0)
         sort_w(0, 0)
-        quantize_x(0, 0, 0, COLS)
+        quantize_pair(0, 0)
+        quantize_pair(1, 0)
         sort_ws(0, 0, 1)
         for q in range(2):
             empty_x(turn_x(q, 1), q, 1)
@@ -308,12 +321,15 @@ def tile_hankel_clipped_response_g4_kernel(
         sort_w(1, 2)
         quantize_x(0, 2, 0, COLS)
         sort_ws(1, 0, KG)
+        PARTS = [[(3, 1), (3, 2)], [(4, 0), (4, 1)], [], [], [], [], [], []]
         turned = [(2, 0), (2, 1), (2, 2), (3, 0)]
         for g in range(1, KG):
             for t in range(PACK):
                 mx_pass(0, t, g)
             for q, gx in turned[2 * g - 2 : 2 * g]:
                 empty_x(turn_x(q, gx), q, gx)
+            for q, gx in PARTS[g - 1]:
+                part_x(nc.scalar.copy, q, gx)
         for t in range(PACK):
             scale_add(0, t)
         for t in range(PACK):
@@ -338,29 +354,31 @@ def tile_hankel_clipped_response_g4_kernel(
                 weave_y(nc.vector.tensor_copy, h - 1, 0, WV)
             scale_add(h, tb)
             clip(h, ta)
+            clip(h, tb)
             if odd:
                 quantize_y(h - 1)
                 store_codes(h - 1)
                 if h % NG == 0:
                     store_scales(h // NG - 1)
-            clip(h, tb)
             j = h // NG + 1
             todo = [(2 * j + i // KG, i % KG) for i in range(2 * KG)]
             turned = todo[2 * (s % 4) : 2 * (s % 4) + 2]
             for q, g in turned:
                 empty_x(turn_x(q, g), q, g)
             out_rows(h - 1, [ta, tb])
+            for q, g in PARTS[s]:
+                part_x(nc.scalar.copy, q, g)
 
         h = halves - 2
         mx_group(h, 0)
         mx_group(h, 1)
-        weave_y(nc.scalar.copy, h - 1, WV, COLS)
-        weave_y(nc.vector.tensor_copy, h - 1, 0, WV)
+        weave_y(nc.scalar.copy, h - 1, 128, COLS)
         scale_add(h, 0)
+        weave_y(nc.vector.tensor_copy, h - 1, 0, 128)
         scale_add(h, 1)
         clip(h, 0)
-        quantize_y(h - 1)
         clip(h, 1)
+        quantize_y(h - 1)
         out_rows(h - 1, range(2))
         store_codes(h - 1)
         store_scales(CHUNKS - 2)
@@ -368,8 +386,8 @@ def tile_hankel_clipped_response_g4_kernel(
         mx_group(h, 2)
         mx_group(h, 3)
         scale_add(h, 2)
-        clip(h, 2)
         scale_add(h, 3)
+        clip(h, 2)
         clip(h, 3)
         h = halves - 1
         mx_group(h, 0)
@@ -396,12 +414,15 @@ def tile_hankel_clipped_response_g4_kernel(
         for t in range(PACK):
             for r in range(RECS):
                 turn_y(h, last_banks[r], r, t)
+        weave_y(nc.scalar.copy, h, 0, C)
         empty_y(nc.scalar.copy, h, last_banks[0], 0)
         empty_y(nc.scalar.copy, h, last_banks[1], 1)
-        weave_y(nc.vector.tensor_copy, h, 0, COLS // 2)
-        weave_y(nc.vector.tensor_copy, h, COLS // 2, COLS)
-        quantize_y(h)
+        weave_y(nc.vector.tensor_copy, h, C, 2 * C)
+        weave_y(nc.vector.tensor_copy, h, 2 * C, COLS)
+        quantize_y(h, 0, 2 * C)
+        quantize_y(h, 2 * C, COLS)
         empty_y(nc.scalar.copy, h, last_banks[2], 2)
-        store_codes(h)
+        store_codes(h, 0, 2 * C)
         empty_y(nc.scalar.copy, h, last_banks[3], 3)
+        store_codes(h, 2 * C, COLS)
         store_scales(CHUNKS - 1)

from contextlib import ExitStack

import concourse.mybir as mybir
from concourse.masks import make_identity

R, C, K, N = 12, 128, 1536, 1024
FLOPS = 2 * R * C * K * N

F32 = mybir.dt.float32
BF16 = mybir.dt.bfloat16
I32 = mybir.dt.int32
U32 = mybir.dt.uint32
U8 = mybir.dt.uint8
FP8X4 = mybir.dt.float8_e4m3fn_x4
FP4X4 = mybir.dt.float4_e2m1fn_x4
ALU = mybir.AluOpType
ACT = mybir.ActivationFunctionType

P = 128
PACK = 4
GROUP = P * PACK
KG = K // GROUP
NG = N // GROUP
RECS = 4
CHUNKS = R // RECS
COLS = RECS * C
BANKS = 8


def tile_hankel_clipped_response_g4_kernel(
    tc, x, hankel_words, hankel_scales, bias, lo, hi, gain, out_0, out_1, out_2
):
    nc = tc.nc
    with ExitStack() as ctx:
        keep = ctx.enter_context(tc.tile_pool(name="keep", bufs=1))
        work = ctx.enter_context(tc.tile_pool(name="work", bufs=4))
        psum = ctx.enter_context(tc.psum_pool(name="psum", bufs=1))
        ctx.enter_context(tc.manual_schedule())

        free_banks = ["bank%d" % b for b in range(BANKS)]
        bank_names = {}

        def next_bank(key):
            name = free_banks.pop(0)
            bank_names[key] = name
            bank = psum.tile([P, COLS], F32, name=name, tag=name)
            return bank

        def release(key):
            free_banks.append(bank_names.pop(key))

        def kept(name, shape, dtype):
            t = keep.tile(shape, dtype, name=name, tag=name, align_bytes=64)
            return t

        ident = kept("ident", [P, P], F32)
        ws_raw = kept("ws_raw", [P, KG, N], U8)
        w_raw = [kept("w_raw%d" % n, [P, KG, 2 * GROUP], U8) for n in range(NG)]
        w_codes = [kept("w_codes%d" % n, [P, KG, PACK, 2 * P], U8) for n in range(NG)]
        w_scales = [kept("w_scales%d" % n, [P, KG, PACK, P], U8) for n in range(NG)]
        x_first = [kept("x_first%d" % g, [P, RECS, GROUP], BF16) for g in range(KG)]
        x_pair = {q: kept("x_pair%d" % q, [P, 2, K], BF16) for q in range(2, R // 2)}
        x_codes = {(j, g): kept("x_codes%d_%d" % (j, g), [P, COLS], U32) for j in range(CHUNKS) for g in range(KG)}
        x_scales = {(j, g): kept("x_scales%d_%d" % (j, g), [P, COLS], U8) for j in range(CHUNKS) for g in range(KG)}
        x_turned = {(j, g): kept("x_turned%d_%d" % (j, g), [P, COLS, 2], F32) for j in range(CHUNKS) for g in range(KG)}
        bias_sb = kept("bias_sb", [P, N], BF16)
        lo_sb = kept("lo_sb", [P, NG * PACK], BF16)
        hi_sb = kept("hi_sb", [P, NG * PACK], BF16)
        gain_sb = kept("gain_sb", [P, NG * PACK], BF16)
        gain32 = kept("gain32", [P, NG * PACK], F32)
        lo_eff = kept("lo_eff", [P, NG * PACK], F32)
        end_a = kept("end_a", [P, NG * PACK], F32)
        end_b = kept("end_b", [P, NG * PACK], F32)
        lower = kept("lower", [P, NG * PACK], F32)
        upper = kept("upper", [P, NG * PACK], F32)
        gain_bias = kept("gain_bias", [P, NG * PACK, C], F32)
        y_scales = [kept("y_scales%d" % j, [P, NG, COLS], U8) for j in range(CHUNKS)]

        def by_lag(vec):
            return vec.rearrange("(n p t) -> p n t", n=NG, t=PACK)

        def load_vec(engine, tile, vec):
            engine.dma_start(out=tile[:].rearrange("p (n t) -> p n t", t=PACK), in_=by_lag(vec))

        def load_w(n, first, last):
            src = hankel_words[first:last, :, 2 * GROUP * n : 2 * GROUP * (n + 1)].rearrange("g p b -> p g b")
            nc.sync.dma_start(out=w_raw[n][:, first:last, :].bitcast(I32), in_=src.bitcast(I32))

        def load_x_first(g, first, last):
            src = x[first:last, :, GROUP * g : GROUP * (g + 1)].rearrange("r c k -> c r k")
            nc.sync.dma_start(out=x_first[g][:, first:last, :], in_=src)

        def load_ws(n):
            lags = slice(GROUP * n, GROUP * (n + 1))
            for q in range(4):
                src = hankel_scales[:, 4 * q : 4 * q + 4, lags].rearrange("g r n -> r g n")
                nc.sync.dma_start(out=ws_raw[32 * q : 32 * q + 4, :, lags].bitcast(I32), in_=src.bitcast(I32))

        nc.vector.memset(ws_raw[:].rearrange("p g n -> p (g n)").bitcast(I32), 0)
        make_identity(nc, ident[:])
        load_vec(nc.scalar, gain_sb, gain)
        load_x_first(0, 0, 2)
        load_x_first(0, 2, RECS)
        load_x_first(1, 0, 2)
        load_w(0, 0, 1)
        load_x_first(1, 2, RECS)
        load_ws(0)
        load_w(0, 1, KG)
        load_x_first(2, 0, RECS)
        nc.sync.dma_start(out=bias_sb[:], in_=bias)
        load_vec(nc.sync, lo_sb, lo)
        load_vec(nc.sync, hi_sb, hi)
        load_w(1, 0, KG)
        load_ws(1)
        for q in range(2, R // 2):
            nc.sync.dma_start(out=x_pair[q][:], in_=x[2 * q : 2 * q + 2, :, :].rearrange("r c k -> c r k"))

        nc.scalar.activation(out=gain32[:], in_=gain_sb[:], func=ACT.Copy)

        def x_words(rec, g):
            if rec < RECS:
                return x_first[g][:, rec, :].bitcast(F32)
            return x_pair[rec // 2][:, rec % 2, GROUP * g : GROUP * (g + 1)].bitcast(F32)

        x_parted = {}

        def part_x(copy, q, g):
            tile = work.tile([P, 2, 2, P], F32, name="x_parted", tag="x_parted", bufs=4)
            x_parted[(q, g)] = tile
            words = x_pair[q][:, :, GROUP * g : GROUP * (g + 1)].bitcast(F32)
            copy(out=tile[:], in_=words.rearrange("c r (p u) -> c r u p", u=2))

        def turn_x(q, g):
            bank = next_bank(("x", q, g))
            for r in range(2):
                for u in range(2):
                    slot = 2 * r + u
                    if (q, g) in x_parted:
                        words = x_parted[(q, g)][:, r, u, :]
                    else:
                        words = x_words(2 * q + r, g)[:, u : 2 * P : 2]
                    nc.tensor.transpose(bank[:, P * slot : P * (slot + 1)], words, ident[:])
            return bank

        def empty_x(bank, q, g):
            half = q % 2
            dst = x_turned[(q // 2, g)][:, 2 * C * half : 2 * C * (half + 1), :]
            nc.scalar.copy(
                out=dst.rearrange("p (r c) u -> p r c u", r=2),
                in_=bank[:].rearrange("p (r u c) -> p r c u", r=2, u=2),
            )
            release(("x", q, g))

        def quantize_x(j, g, first, last):
            cols = slice(first, last)
            nc.vector.quantize_mx(
                out=x_codes[(j, g)][:, cols].bitcast(FP8X4),
                scales=x_scales[(j, g)][:, cols],
                in_=x_turned[(j, g)][:, cols, :].rearrange("p m u -> p (m u)").bitcast(BF16),
            )

        def sort_w(n, g):
            nc.vector.tensor_copy(
                out=w_codes[n][:, g, :, :].rearrange("p t (m b) -> p t m b", b=2),
                in_=w_raw[n][:, g, :].rearrange("p (m t b) -> p t m b", t=PACK, b=2),
            )

        def sort_ws(n, first, last):
            nc.vector.tensor_copy(
                out=w_scales[n][:, first:last, :, :],
                in_=ws_raw[:, first:last, GROUP * n : GROUP * (n + 1)].rearrange("p g (m t) -> p g t m", t=PACK),
            )

        acc = {}
        pre = {}
        y_lag = {}
        y_bf = {}
        y_codes = {}

        def mx_pass(h, t, g):
            j, n = divmod(h, NG)
            if g == 0:
                acc[(h, t)] = next_bank(("z", h, t))
            nc.tensor.matmul_mx(
                out=acc[(h, t)][:],
                lhsT=w_codes[n][:, g, t, :].bitcast(FP4X4),
                lhsT_scale=w_scales[n][:, g, t, :],
                rhs=x_codes[(j, g)][:].bitcast(FP8X4),
                rhs_scale=x_scales[(j, g)][:],
                start=(g == 0),
                stop=(g == KG - 1),
            )

        def mx_group(h, t):
            for g in range(KG):
                mx_pass(h, t, g)

        def scale_add(h, t, first=0, last=RECS):
            lag = PACK * (h % NG) + t
            if (h, t) not in pre:
                tile = work.tile([P, RECS, C], F32, name="pre", tag="pre")
                pre[(h, t)] = tile
            nc.vector.scalar_tensor_tensor(
                out=pre[(h, t)][:, first:last, :],
                in0=acc[(h, t)][:].rearrange("p (r c) -> p r c", r=RECS)[:, first:last, :],
                scalar=gain32[:, lag : lag + 1],
                in1=gain_bias[:, lag, :].unsqueeze(1).to_broadcast([P, last - first, C]),
                op0=ALU.mult,
                op1=ALU.add,
            )
            if last == RECS:
                release(("z", h, t))

        def clip(h, t, first=0, last=RECS):
            lag = PACK * (h % NG) + t
            if h not in y_lag:
                tile = work.tile([P, PACK, COLS], F32, name="y_lag", tag="y_lag", bufs=3)
                y_lag[h] = tile
            nc.vector.tensor_scalar(
                out=y_lag[h][:, t, C * first : C * last],
                in0=pre[(h, t)][:, first:last, :].rearrange("p r c -> p (r c)"),
                scalar1=upper[:, lag : lag + 1],
                scalar2=lower[:, lag : lag + 1],
                op0=ALU.min,
                op1=ALU.max,
            )

        def turn_y(h, bank, r, t):
            nc.tensor.transpose(bank[:, P * t : P * (t + 1)], y_lag[h][:, t, C * r : C * (r + 1)], ident[:])

        def empty_y(copy, h, bank, r):
            j, n = divmod(h, NG)
            y_row = work.tile([P, GROUP], F32, name="y_row", tag="y_row", bufs=6)
            copy(
                out=y_row[:].rearrange("c (p t) -> c p t", t=PACK),
                in_=bank[:].rearrange("c (t p) -> c p t", t=PACK),
            )
            release(("y", h, r))
            nc.sync.dma_start(out=out_0[RECS * j + r, :, GROUP * n : GROUP * (n + 1)], in_=y_row[:])

        def weave_y(copy, h, first, last):
            if h not in y_bf:
                tile = work.tile([P, COLS, PACK], BF16, name="y_bf", tag="y_bf", bufs=2, align_bytes=64)
                y_bf[h] = tile
            copy(
                out=y_bf[h][:, first:last, :].rearrange("p (c i) t -> p c t i", i=4),
                in_=y_lag[h][:, :, first:last].rearrange("p t (c i) -> p c t i", i=4),
            )

        def quantize_y(h, first=0, last=COLS):
            j, n = divmod(h, NG)
            if h not in y_codes:
                y_codes[h] = kept("y_codes%d" % h, [P, COLS], U32)
            codes = y_codes[h][:, first:last]
            nc.vector.quantize_mx(
                out=codes.bitcast(FP8X4),
                scales=y_scales[j][:, n, first:last],
                in_=y_bf[h][:, first:last, :].rearrange("p m t -> p (m t)"),
            )

        def store_codes(h, first=0, last=COLS):
            j, n = divmod(h, NG)
            dst = out_1[n, :, COLS * j + first : COLS * j + last, :].rearrange("p m t -> p (m t)")
            nc.sync.dma_start(out=dst.bitcast(I32), in_=y_codes[h][:, first:last].bitcast(I32))

        def store_scales(j):
            for q in range(4):
                dst = out_2[:, 4 * q : 4 * q + 4, COLS * j : COLS * (j + 1)].rearrange("n r m -> r n m")
                nc.sync.dma_start(out=dst.bitcast(I32), in_=y_scales[j][32 * q : 32 * q + 4, :, :].bitcast(I32))

        def out_rows(h, records):
            for r in records:
                bank = next_bank(("y", h, r))
                for t in range(PACK):
                    turn_y(h, bank, r, t)
                empty_y(nc.scalar.copy, h, bank, r)

        def quantize_pair(q, g):
            quantize_x(q // 2, g, 2 * C * (q % 2), 2 * C * (q % 2 + 1))

        for q in range(2):
            empty_x(turn_x(q, 0), q, 0)
        sort_w(0, 0)
        quantize_pair(0, 0)
        quantize_pair(1, 0)
        sort_ws(0, 0, 1)
        for q in range(2):
            empty_x(turn_x(q, 1), q, 1)
        sort_ws(0, 1, KG)
        sort_w(0, 1)
        quantize_x(0, 1, 0, COLS)
        sort_w(0, 2)
        for t in range(PACK):
            mx_pass(0, t, 0)
        for q in range(2):
            empty_x(turn_x(q, 2), q, 2)
        bias_bank = next_bank("bias")
        bias_words = bias_sb[:].bitcast(F32)
        for n in range(NG):
            for u in range(2):
                slot = 2 * n + u
                nc.tensor.transpose(
                    bias_bank[:, P * slot : P * (slot + 1)], bias_words[:, 2 * P * n + u : 2 * P * (n + 1) : 2], ident[:]
                )
        bias_by_lag = bias_bank[:].bitcast(BF16).rearrange("p (s c e) -> p s e c", c=C, e=2)
        for lag in range(NG * PACK):
            nc.scalar.activation(
                out=gain_bias[:, lag, :],
                in_=bias_by_lag[:, lag // 2, lag % 2, :],
                func=ACT.Copy,
                scale=gain32[:, lag : lag + 1],
            )
        release("bias")
        nc.vector.tensor_tensor(out=lo_eff[:], in0=lo_sb[:], in1=hi_sb[:], op=ALU.min)
        nc.vector.tensor_tensor(out=end_b[:], in0=hi_sb[:], in1=gain32[:], op=ALU.mult)
        sort_w(1, 0)
        nc.vector.tensor_tensor(out=end_a[:], in0=lo_eff[:], in1=gain32[:], op=ALU.mult)
        sort_w(1, 1)
        nc.vector.tensor_tensor(out=lower[:], in0=end_a[:], in1=end_b[:], op=ALU.min)
        nc.vector.tensor_tensor(out=upper[:], in0=end_a[:], in1=end_b[:], op=ALU.max)
        sort_w(1, 2)
        quantize_x(0, 2, 0, COLS)
        sort_ws(1, 0, KG)
        PARTS = [[(3, 1), (3, 2)], [(4, 0), (4, 1)], [], [], [], [], [], []]
        turned = [(2, 0), (2, 1), (2, 2), (3, 0)]
        for g in range(1, KG):
            for t in range(PACK):
                mx_pass(0, t, g)
            for q, gx in turned[2 * g - 2 : 2 * g]:
                empty_x(turn_x(q, gx), q, gx)
            for q, gx in PARTS[g - 1]:
                part_x(nc.scalar.copy, q, gx)
        for t in range(PACK):
            scale_add(0, t)
        for t in range(PACK):
            clip(0, t)

        halves = CHUNKS * NG
        WV = 128
        WM = (WV + COLS) // 2
        for s in range(2, 2 * halves - 4):
            h, odd = divmod(s, 2)
            ta, tb = 2 * odd, 2 * odd + 1
            mx_group(h, ta)
            mx_group(h, tb)
            if not odd:
                weave_y(nc.scalar.copy, h - 1, WV, WM)
            else:
                weave_y(nc.scalar.copy, h - 1, WM, COLS)
            for q, g in turned:
                quantize_pair(q, g)
            scale_add(h, ta)
            if not odd:
                weave_y(nc.vector.tensor_copy, h - 1, 0, WV)
            scale_add(h, tb)
            clip(h, ta)
            clip(h, tb)
            if odd:
                quantize_y(h - 1)
                store_codes(h - 1)
                if h % NG == 0:
                    store_scales(h // NG - 1)
            j = h // NG + 1
            todo = [(2 * j + i // KG, i % KG) for i in range(2 * KG)]
            turned = todo[2 * (s % 4) : 2 * (s % 4) + 2]
            for q, g in turned:
                empty_x(turn_x(q, g), q, g)
            out_rows(h - 1, [ta, tb])
            for q, g in PARTS[s]:
                part_x(nc.scalar.copy, q, g)

        h = halves - 2
        mx_group(h, 0)
        mx_group(h, 1)
        weave_y(nc.scalar.copy, h - 1, 128, COLS)
        scale_add(h, 0)
        weave_y(nc.vector.tensor_copy, h - 1, 0, 128)
        scale_add(h, 1)
        clip(h, 0)
        clip(h, 1)
        quantize_y(h - 1)
        out_rows(h - 1, range(2))
        store_codes(h - 1)
        store_scales(CHUNKS - 2)
        out_rows(h - 1, range(2, RECS))
        mx_group(h, 2)
        mx_group(h, 3)
        scale_add(h, 2)
        scale_add(h, 3)
        clip(h, 2)
        clip(h, 3)
        h = halves - 1
        mx_group(h, 0)
        mx_group(h, 1)
        weave_y(nc.scalar.copy, h - 1, 192, COLS)
        scale_add(h, 0)
        weave_y(nc.vector.tensor_copy, h - 1, 0, 192)
        scale_add(h, 1)
        clip(h, 0)
        quantize_y(h - 1)
        clip(h, 1)
        out_rows(h - 1, range(1))
        store_codes(h - 1)
        out_rows(h - 1, range(1, RECS))
        mx_group(h, 2)
        mx_group(h, 3)
        scale_add(h, 2)
        scale_add(h, 3, 0, 2)
        clip(h, 2)
        clip(h, 3, 0, 2)
        scale_add(h, 3, 2, 4)
        clip(h, 3, 2, 4)
        last_banks = [next_bank(("y", h, r)) for r in range(RECS)]
        for t in range(PACK):
            for r in range(RECS):
                turn_y(h, last_banks[r], r, t)
        weave_y(nc.scalar.copy, h, 0, C)
        empty_y(nc.scalar.copy, h, last_banks[0], 0)
        empty_y(nc.scalar.copy, h, last_banks[1], 1)
        weave_y(nc.vector.tensor_copy, h, C, 2 * C)
        weave_y(nc.vector.tensor_copy, h, 2 * C, COLS)
        quantize_y(h, 0, 2 * C)
        quantize_y(h, 2 * C, COLS)
        empty_y(nc.scalar.copy, h, last_banks[2], 2)
        store_codes(h, 0, 2 * C)
        empty_y(nc.scalar.copy, h, last_banks[3], 3)
        store_codes(h, 2 * C, COLS)
        store_scales(CHUNKS - 1)
